import numpy as np
import ml_dtypes


def mxq(x, axis, fmt="e4m3"):
    dtype, down = {"e4m3": (ml_dtypes.float8_e4m3fn, 7), "e5m2": (ml_dtypes.float8_e5m2, 14)}[fmt]
    v = np.moveaxis(np.asarray(x, np.float32).astype(ml_dtypes.bfloat16).astype(np.float64), axis, -1)
    blocks = v.reshape(v.shape[:-1] + (-1, 32))
    amax = np.abs(blocks).max(-1, keepdims=True)
    byte = np.maximum(np.where(amax > 0, np.frexp(amax)[1] - 1 + 127, 0) - down, 1)
    scale = np.exp2(byte - 127.0)
    codes = (blocks / scale).astype(np.float32).astype(dtype).astype(np.float64)
    return np.moveaxis((codes * scale).reshape(v.shape), -1, axis)


WIDE = False


def mx_kscale(k):
    if not WIDE:
        return np.ones(k)
    levels = np.array([10, -10, 5, -5, 0])
    if k % 512:
        return np.exp2(np.random.permutation(np.resize(levels, k // 32))).repeat(32)
    a = np.empty((k // 512, 16))
    for p in range(k // 512):
        a[p, :8] = np.random.permutation(np.resize(levels, 8))
        for g in range(8):
            far = levels[np.abs(levels - a[p, g]) >= 10]
            a[p, g + 8] = far[np.random.randint(len(far))]
    return np.exp2(a.ravel()).repeat(32)


BF16 = ml_dtypes.bfloat16


def bf(x):
    return np.asarray(x, np.float32).astype(BF16)


def f64(x):
    return np.asarray(x).astype(np.float64)


E2M1 = np.array([0.0, 0.5, 1.0, 1.5, 2.0, 3.0, 4.0, 6.0, -0.0, -0.5, -1.0, -1.5, -2.0, -3.0, -4.0, -6.0])


def pack_weight(w, fmt):
    k, n = w.shape
    w = f64(bf(w)).reshape(k // 32, 32, n)
    amax = np.abs(w).max(1)
    if fmt == "e4m3":
        byte = np.frexp(amax)[1] - 1 + 127 - 7
    else:
        mant, ex = np.frexp(amax / 6.0)
        byte = np.where(mant > 0.5, ex, ex - 1) + 127
    byte = np.clip(np.where(amax > 0, byte, 1), 1, 254)
    scaled = (w * np.exp2(127.0 - byte)[:, None, :]).reshape(k, n).astype(np.float32)
    by_word = np.ascontiguousarray(scaled.reshape(k // 512, 128, 4, n).transpose(0, 1, 3, 2))
    if fmt == "e4m3":
        words = by_word.astype(ml_dtypes.float8_e4m3fn).view(np.uint8)
    else:
        c = by_word.astype(ml_dtypes.float4_e2m1fn).view(np.uint8) & 0xF
        words = c[..., 0::2] | (c[..., 1::2] << 4)
    return np.ascontiguousarray(words), np.ascontiguousarray(byte.astype(np.uint8).reshape(k // 512, 16, n))


def unpack_weight(words, scales, fmt):
    g, p, n, _ = words.shape
    if fmt == "e4m3":
        vals = np.ascontiguousarray(words).view(ml_dtypes.float8_e4m3fn).astype(np.float64)
    else:
        nib = np.empty((g, p, n, 4), np.uint8)
        nib[..., 0::2] = words & 0xF
        nib[..., 1::2] = words >> 4
        vals = E2M1[nib]
    vals = vals * np.repeat(np.exp2(scales.astype(np.float64) - 127.0), 8, axis=1)[..., None]
    return vals.transpose(0, 1, 3, 2).reshape(g * 512, n)
def pack4(w):
    words, scales = pack_weight(w, "e2m1")
    return words.reshape(words.shape[0], 128, -1), scales


def unpack4(words, scales):
    return unpack_weight(words.reshape(words.shape[0], 128, -1, 2), scales, "e2m1")


C, A, U, L = 1536, 1024, 512, 1024


def draw0():
    s, r, t = mx_kscale(A), mx_kscale(U), mx_kscale(L)
    d_words, d_scales = pack4(np.random.standard_normal((A, L)) / np.sqrt(A) / s[:, None])
    m_words, m_scales = pack4(np.random.standard_normal((L, A)) / np.sqrt(L) / t[:, None])
    return {"psi": bf(np.random.standard_normal((C, A)) * s),
            "ray": bf(np.random.standard_normal((C, U)) * r),
            "d_words": d_words,
            "d_scales": d_scales,
            "e": bf(np.random.standard_normal((U, L)) / np.sqrt(U) / r[:, None]),
            "sigma": bf(np.random.uniform(0.3, 1.2, (C, L)) * t),
            "ext": bf(0.4 * np.random.standard_normal((C, L)) * t),
            "m_words": m_words,
            "m_scales": m_scales}


def core(psi, ray, d_words, d_scales, e, sigma, ext, m_words, m_scales):
    D = unpack4(d_words, d_scales)
    M = unpack4(m_words, m_scales)
    phi = ((mxq(f64(psi), 1, "e4m3") @ D)
           + (mxq(f64(ray), 1, "e4m3") @ mxq(f64(e), 0, "e4m3")))
    src = phi * f64(sigma) + f64(ext)
    return mxq(src, 1, "e4m3") @ M


def e4m3fn_bytes(y):
    return np.clip(np.asarray(y, np.float64), -448.0, 448.0).astype(np.float32).astype(ml_dtypes.float8_e4m3fn).view(np.uint8)


def e4m3fn_values(b):
    return np.asarray(b, np.uint8).view(ml_dtypes.float8_e4m3fn).astype(np.float64)


def setup_inputs():
    d = draw0()
    x0 = np.asarray(d['psi']).astype(np.float64)
    s = (np.max(np.abs(x0), axis=(0,), keepdims=True) / 448.0).astype(np.float32)
    out = {}
    for k, v in d.items():
        if k == 'psi':
            out['psi_bytes'] = e4m3fn_bytes(x0 / s.astype(np.float64))
            out['psi_scale'] = s
        else:
            out[k] = v
    return out


def reference(psi_bytes, psi_scale, ray, d_words, d_scales, e, sigma, ext, m_words, m_scales):
    return core(e4m3fn_values(psi_bytes) * psi_scale.astype(np.float64), ray, d_words, d_scales, e, sigma, ext, m_words, m_scales)

@@ -1,0 +1,341 @@
+from contextlib import ExitStack
+
+import concourse.mybir as mybir
+from concourse.masks import make_identity
+
+C, A, U, L = 1536, 1024, 512, 1024
+FLOPS = 2 * C * L * (A + U + A)
+
+F32 = mybir.dt.float32
+BF16 = mybir.dt.bfloat16
+U32 = mybir.dt.uint32
+I32 = mybir.dt.int32
+U8 = mybir.dt.uint8
+E4M3 = mybir.dt.float8_e4m3fn
+FP8X4 = mybir.dt.float8_e4m3fn_x4
+FP4X4 = mybir.dt.float4_e2m1fn_x4
+MULT = mybir.AluOpType.mult
+ADD = mybir.AluOpType.add
+
+P = 128
+NT = C // P
+H = 512
+
+
+def tile_ordinates_scattering_source_s3_kernel(
+    tc, psi_bytes, psi_scale, ray, d_words, d_scales, e, sigma, ext, m_words, m_scales, out
+):
+    nc = tc.nc
+    psi_v = psi_bytes.rearrange("(p i) a -> p i a", i=NT)
+    ray_v = ray.rearrange("(p i) a -> p i a", i=NT)
+    sig_v = sigma.rearrange("(p i) a -> p i a", i=NT)
+    ext_v = ext.rearrange("(p i) a -> p i a", i=NT)
+    out_v = out.rearrange("(p i) a -> p i a", i=NT)
+    e_v = e.rearrange("(p j) n -> p j n", j=4)
+
+    with ExitStack() as ctx:
+        keep = ctx.enter_context(tc.tile_pool(name="keep", bufs=1))
+        work = ctx.enter_context(tc.tile_pool(name="work", bufs=3))
+        psum = ctx.enter_context(tc.psum_pool(name="psum", bufs=1))
+        ctx.enter_context(tc.manual_schedule())
+
+        ident = keep.tile([P, P], F32, name="ident")
+        make_identity(nc, ident[:])
+        warm = keep.tile([P, 8], F32, name="warm")
+        nc.gpsimd.memset(warm[:], 0.0)
+        warm2 = keep.tile([P, 8], F32, name="warm2")
+        nc.scalar.copy(out=warm2[:], in_=warm[:])
+
+        ds = keep.tile([P, 2, L], U8, name="ds", align_bytes=256)
+        ms = keep.tile([P, 2, A], U8, name="ms", align_bytes=256)
+        nc.vector.memset(ds[:].bitcast(I32), 0)
+        nc.vector.memset(ms[:].bitcast(I32), 0)
+
+        psi_t, ray_t, sig_t, ext_t = {}, {}, {}, {}
+
+        def load(store, view, dt, width, i0, n, nm):
+            t = keep.tile([P, n, width], dt, name=nm + str(i0), align_bytes=64)
+            nc.sync.dma_start(out=t[:], in_=view[:, i0 : i0 + n, :])
+            for k in range(n):
+                store[i0 + k] = t[:, k, :]
+
+        def load_psi(i0, n):
+            load(psi_t, psi_v, U8, A, i0, n, "psib")
+
+        def load_ray(i0, n):
+            load(ray_t, ray_v, BF16, U, i0, n, "ray")
+
+        def load_se(i0, n):
+            load(sig_t, sig_v, BF16, L, i0, n, "sig")
+            load(ext_t, ext_v, BF16, L, i0, n, "ext")
+
+        def load_scales(t, src):
+            for q in range(4):
+                nc.sync.dma_start(
+                    out=t[32 * q : 32 * q + 4, :, :].bitcast(I32),
+                    in_=src[:, 4 * q : 4 * q + 4, :].rearrange("g q n -> q g n").bitcast(I32),
+                )
+
+        sc = keep.tile([P, 2, 4], F32, name="sc")
+        nc.scalar.dma_start(out=sc[:], in_=psi_scale.rearrange("o (g p t) -> p (o g) t", p=P, t=4))
+        load_psi(0, 1)
+        load_ray(0, 2)
+        dw = keep.tile([P, 2, 2 * L], U8, name="dw", align_bytes=256)
+        nc.sync.dma_start(out=dw[:], in_=d_words.rearrange("g p n -> p g n"))
+        load_scales(ds, d_scales)
+        load_psi(1, 1)
+        e_raw = []
+        for h in range(2):
+            t = keep.tile([P, 4, H], BF16, name="eraw" + str(h), align_bytes=64)
+            nc.sync.dma_start(out=t[:], in_=e_v[:, :, H * h : H * (h + 1)])
+            e_raw.append(t)
+        load_se(0, 1)
+        load_psi(2, 2)
+        load_ray(2, 2)
+        load_se(1, 1)
+        mw = keep.tile([P, 2, 2 * A], U8, name="mw", align_bytes=256)
+        nc.sync.dma_start(out=mw[:], in_=m_words.rearrange("g p n -> p g n"))
+        load_scales(ms, m_scales)
+        load_se(2, 2)
+        load_psi(4, 4)
+        load_ray(4, 4)
+        load_se(4, 2)
+        load_psi(8, 4)
+        load_ray(8, 4)
+        for i in range(6, NT, 2):
+            load_se(i, 2)
+
+        eq = [keep.tile([P, H], U32, name="eq" + str(h), align_bytes=256) for h in range(2)]
+        es = [keep.tile([P, H], U8, name="es" + str(h), align_bytes=256) for h in range(2)]
+        eg = [keep.tile([P, 4 * H], BF16, name="eg" + str(h), align_bytes=256) for h in range(2)]
+
+        def e_part(copy, h, c0, c1):
+            copy(
+                out=eg[h][:, 4 * c0 : 4 * c1].rearrange("p (c i t) -> p c t i", i=4, t=4),
+                in_=e_raw[h][:, :, c0:c1].rearrange("p t (c i) -> p c t i", i=4),
+            )
+
+        def e_quant(h):
+            nc.vector.quantize_mx(out=eq[h][:].bitcast(FP8X4), scales=es[h][:], in_=eg[h][:])
+
+        pb, pt, pg, pq, rt, rg, rq, acc, tt, sp, st, sg, sq, oacc, ot = ({} for x in range(15))
+
+        def cast(i):
+            t = work.tile([P, A], BF16, name="pb", align_bytes=64)
+            pb[i] = t
+            nc.scalar.copy(out=t[:], in_=psi_t[i].bitcast(E4M3))
+
+        def tr_psi(i):
+            t = psum.tile([P, 4, P], F32, name="pt", bufs=2)
+            pt[i] = t
+            words = pb[i][:].bitcast(F32)
+            for g in range(2):
+                for u in range(2):
+                    nc.tensor.transpose(t[:, 2 * g + u, :], words[:, 256 * g + u : 256 * (g + 1) : 2], ident[:])
+
+        def tr_ray(i):
+            t = psum.tile([P, 2, P], F32, name="rt", bufs=1)
+            rt[i] = t
+            words = ray_t[i].bitcast(F32)
+            for u in range(2):
+                nc.tensor.transpose(t[:, u, :], words[:, u:256:2], ident[:])
+
+        def scale_psi(i, g):
+            if g == 0:
+                t = work.tile([P, 2, H], BF16, name="pg", align_bytes=64)
+                pg[i] = t
+            t = pg[i]
+            bank = pt[i][:].rearrange("p s r -> p (s r)").bitcast(BF16)
+            nc.vector.tensor_tensor(
+                out=t[:, g, :].rearrange("p (r u e) -> p r u e", u=2, e=2),
+                in0=bank[:, H * g : H * (g + 1)].rearrange("p (u r e) -> p r u e", u=2, e=2),
+                in1=sc[:, g, :].unsqueeze(1).to_broadcast([P, P, 4]).rearrange("p r (u e) -> p r u e", u=2, e=2),
+                op=MULT,
+            )
+
+        def quant(store, i, src, words, nm):
+            q = work.tile([P, words], U32, name=nm + "q", align_bytes=64)
+            s = work.tile([P, words], U8, name=nm + "s", align_bytes=64)
+            store[i] = (q, s)
+            nc.vector.quantize_mx(out=q[:].bitcast(FP8X4), scales=s[:], in_=src)
+
+        def q_psi(i):
+            quant(pq, i, pg[i][:].rearrange("p g n -> p (g n)"), 256, "p")
+
+        def q_ray(i):
+            quant(rq, i, rg[i][:], 128, "r")
+
+        def q_src(i):
+            quant(sq, i, sg[i][:], 256, "s")
+
+        def ray_evac(i):
+            t = work.tile([P, U], BF16, name="rg", align_bytes=64)
+            rg[i] = t
+            nc.scalar.copy(
+                out=t[:].bitcast(F32).rearrange("p (r u) -> p r u", u=2),
+                in_=rt[i][:].rearrange("p u r -> p r u"),
+            )
+
+        def phi_pass(i, n, k):
+            if k == 0:
+                acc[i, n] = psum.tile([P, H], F32, name="acc", bufs=2)
+            cols = slice(H * n, H * (n + 1))
+            if k < 2:
+                q, s = pq[i]
+                lq, ls = q[:, P * k : P * (k + 1)], s[:, P * k : P * (k + 1)]
+                r = dw[:, k, 2 * H * n : 2 * H * (n + 1)].bitcast(FP4X4)
+                rs = ds[:, k, cols]
+            else:
+                q, s = rq[i]
+                lq, ls = q[:], s[:]
+                r = eq[n][:].bitcast(FP8X4)
+                rs = es[n][:]
+            nc.tensor.matmul_mx(
+                out=acc[i, n][:], lhsT=lq.bitcast(FP8X4), lhsT_scale=ls, rhs=r, rhs_scale=rs, start=(k == 0), stop=(k == 2)
+            )
+
+        def phi(i, n):
+            for k in range(3):
+                phi_pass(i, n, k)
+
+        def mul_sigma(i, n):
+            t = work.tile([P, H], F32, name="t" + str(n), align_bytes=64)
+            tt[i, n] = t
+            nc.vector.tensor_tensor(out=t[:], in0=acc[i, n][:], in1=sig_t[i][:, H * n : H * (n + 1)], op=MULT)
+
+        def add_ext(i, n):
+            t = work.tile([P, H], BF16, name="sp" + str(n), align_bytes=64)
+            sp[i, n] = t
+            eng = nc.gpsimd if n == 0 else nc.vector
+            eng.tensor_tensor(
+                out=t[:].rearrange("p (u q e) -> p u q e", u=2, e=2),
+                in0=tt[i, n][:].rearrange("p (q u e) -> p u q e", u=2, e=2),
+                in1=ext_t[i][:, H * n : H * (n + 1)].rearrange("p (q u e) -> p u q e", u=2, e=2),
+                op=ADD,
+            )
+
+        def tr_src(i):
+            t = psum.tile([P, 4, P], F32, name="st", bufs=1)
+            st[i] = t
+            for n in range(2):
+                words = sp[i, n][:].bitcast(F32)
+                for u in range(2):
+                    nc.tensor.transpose(t[:, 2 * n + u, :], words[:, P * u : P * (u + 1)], ident[:])
+
+        def src_evac(i):
+            t = work.tile([P, L], BF16, name="sg", align_bytes=64)
+            sg[i] = t
+            nc.scalar.copy(
+                out=t[:].bitcast(F32).rearrange("p (n r u) -> p n r u", n=2, u=2),
+                in_=st[i][:].rearrange("p (n u) r -> p n r u", n=2),
+            )
+
+        def out_mm(i, n):
+            o = psum.tile([P, H], F32, name="oacc", bufs=2)
+            oacc[i, n] = o
+            q, s = sq[i]
+            for g in range(2):
+                nc.tensor.matmul_mx(
+                    out=o[:],
+                    lhsT=q[:, P * g : P * (g + 1)].bitcast(FP8X4),
+                    lhsT_scale=s[:, P * g : P * (g + 1)],
+                    rhs=mw[:, g, 2 * H * n : 2 * H * (n + 1)].bitcast(FP4X4),
+                    rhs_scale=ms[:, g, H * n : H * (n + 1)],
+                    start=(g == 0),
+                    stop=(g == 1),
+                )
+
+        def out_evac(i, n):
+            if n == 0:
+                t = work.tile([P, A], F32, name="ot", align_bytes=64)
+                ot[i] = t
+            t = ot[i]
+            nc.scalar.copy(out=t[:, H * n : H * (n + 1)], in_=oacc[i, n][:])
+            if i == NT - 1:
+                nc.sync.dma_start(out=out_v[:, i, H * n : H * (n + 1)], in_=t[:, H * n : H * (n + 1)])
+            elif n == 1:
+                nc.sync.dma_start(out=out_v[:, i, :], in_=t[:])
+
+        def ok(i):
+            return 0 <= i < NT
+
+        cast(0)
+        tr_psi(0)
+        tr_ray(0)
+        scale_psi(0, 0)
+        ray_evac(0)
+        scale_psi(0, 1)
+        q_ray(0)
+        q_psi(0)
+        cast(1)
+        tr_psi(1)
+        tr_ray(1)
+        ray_evac(1)
+        e_part(nc.vector.tensor_copy, 0, 0, 256)
+        e_part(nc.scalar.copy, 0, 256, 512)
+        scale_psi(1, 0)
+        e_quant(0)
+        e_part(nc.vector.tensor_copy, 1, 0, 256)
+        e_part(nc.scalar.copy, 1, 256, 512)
+        scale_psi(1, 1)
+        e_quant(1)
+        q_psi(1)
+        q_ray(1)
+        for k in range(2):
+            for n in range(2):
+                phi_pass(0, n, k)
+        for n in range(2):
+            phi_pass(0, n, 2)
+        cast(2)
+
+        for s in range(NT + 3):
+            if s == 0:
+                mul_sigma(0, 0)
+                add_ext(0, 0)
+                mul_sigma(0, 1)
+                phi(1, 0)
+                phi(1, 1)
+                tr_psi(2)
+                tr_ray(2)
+                ray_evac(2)
+                cast(3)
+                scale_psi(2, 0)
+                continue
+            if ok(s + 2):
+                tr_psi(s + 2)
+                tr_ray(s + 2)
+            if ok(s - 2):
+                tr_src(s - 2)
+            if ok(s + 1):
+                scale_psi(s + 1, 1)
+            if ok(s - 1):
+                add_ext(s - 1, 1)
+            if ok(s - 3):
+                out_evac(s - 3, 1)
+            if ok(s + 2):
+                ray_evac(s + 2)
+            if ok(s + 1):
+                q_psi(s + 1)
+            if s == 1:
+                q_ray(2)
+            if ok(s + 2):
+                q_ray(s + 2)
+            if ok(s - 2):
+                src_evac(s - 2)
+                q_src(s - 2)
+            if ok(s) and s > 1:
+                phi(s, 0)
+                phi(s, 1)
+            if ok(s + 3):
+                cast(s + 3)
+            if ok(s):
+                mul_sigma(s, 0)
+                add_ext(s, 0)
+            if ok(s + 2):
+                scale_psi(s + 2, 0)
+            if ok(s):
+                mul_sigma(s, 1)
+            if ok(s - 2):
+                out_mm(s - 2, 0)
+                out_mm(s - 2, 1)
+                out_evac(s - 2, 0)

@@ -19,6 +19,8 @@ ADD = mybir.AluOpType.add
 
 P = 128
 NT = C // P
+ES0 = 256
+ES1 = 320
 H = 512
 
 
@@ -35,10 +37,12 @@ def tile_ordinates_scattering_source_s3_kernel(
 
     with ExitStack() as ctx:
         keep = ctx.enter_context(tc.tile_pool(name="keep", bufs=1))
-        work = ctx.enter_context(tc.tile_pool(name="work", bufs=3))
+        work = ctx.enter_context(tc.tile_pool(name="work", bufs=4))
         psum = ctx.enter_context(tc.psum_pool(name="psum", bufs=1))
         ctx.enter_context(tc.manual_schedule())
 
+        sc = keep.tile([P, 2, 4], F32, name="sc")
+        nc.scalar.dma_start(out=sc[:], in_=psi_scale.rearrange("o (g p t) -> p (o g) t", p=P, t=4))
         ident = keep.tile([P, P], F32, name="ident")
         make_identity(nc, ident[:])
         warm = keep.tile([P, 8], F32, name="warm")
@@ -76,29 +80,32 @@ def tile_ordinates_scattering_source_s3_kernel(
                     in_=src[:, 4 * q : 4 * q + 4, :].rearrange("g q n -> q g n").bitcast(I32),
                 )
 
-        sc = keep.tile([P, 2, 4], F32, name="sc")
-        nc.scalar.dma_start(out=sc[:], in_=psi_scale.rearrange("o (g p t) -> p (o g) t", p=P, t=4))
-        load_psi(0, 1)
-        load_ray(0, 2)
+        load_psi(0, 2)
+        load_scales(ds, d_scales)
         dw = keep.tile([P, 2, 2 * L], U8, name="dw", align_bytes=256)
         nc.sync.dma_start(out=dw[:], in_=d_words.rearrange("g p n -> p g n"))
-        load_scales(ds, d_scales)
-        load_psi(1, 1)
         e_raw = []
-        for h in range(2):
+
+        def load_e(h):
             t = keep.tile([P, 4, H], BF16, name="eraw" + str(h), align_bytes=64)
             nc.sync.dma_start(out=t[:], in_=e_v[:, :, H * h : H * (h + 1)])
             e_raw.append(t)
-        load_se(0, 1)
+
+        load_e(0)
+        load_ray(0, 2)
         load_psi(2, 2)
+        load_e(1)
+        load_se(0, 1)
         load_ray(2, 2)
         load_se(1, 1)
+        load_psi(4, 2)
+        load_ray(4, 2)
         mw = keep.tile([P, 2, 2 * A], U8, name="mw", align_bytes=256)
         nc.sync.dma_start(out=mw[:], in_=m_words.rearrange("g p n -> p g n"))
         load_scales(ms, m_scales)
         load_se(2, 2)
-        load_psi(4, 4)
-        load_ray(4, 4)
+        load_psi(6, 2)
+        load_ray(6, 2)
         load_se(4, 2)
         load_psi(8, 4)
         load_ray(8, 4)
@@ -120,10 +127,16 @@ def tile_ordinates_scattering_source_s3_kernel(
 
         pb, pt, pg, pq, rt, rg, rq, acc, tt, sp, st, sg, sq, oacc, ot = ({} for x in range(15))
 
-        def cast(i):
+        def cast_tile(i):
             t = work.tile([P, A], BF16, name="pb", align_bytes=64)
             pb[i] = t
-            nc.scalar.copy(out=t[:], in_=psi_t[i].bitcast(E4M3))
+
+        def cast_part(copy, i, a, b):
+            copy(out=pb[i][:, a:b], in_=psi_t[i][:, a:b].bitcast(E4M3))
+
+        def cast(i):
+            cast_tile(i)
+            cast_part(nc.scalar.copy, i, 0, A)
 
         def tr_psi(i):
             t = psum.tile([P, 4, P], F32, name="pt", bufs=2)
@@ -133,8 +146,8 @@ def tile_ordinates_scattering_source_s3_kernel(
                 for u in range(2):
                     nc.tensor.transpose(t[:, 2 * g + u, :], words[:, 256 * g + u : 256 * (g + 1) : 2], ident[:])
 
-        def tr_ray(i):
-            t = psum.tile([P, 2, P], F32, name="rt", bufs=1)
+        def tr_ray(i, tag="rt"):
+            t = psum.tile([P, 2, P], F32, name=tag, bufs=1)
             rt[i] = t
             words = ray_t[i].bitcast(F32)
             for u in range(2):
@@ -168,6 +181,16 @@ def tile_ordinates_scattering_source_s3_kernel(
         def q_src(i):
             quant(sq, i, sg[i][:], 256, "s")
 
+        def q_src_half(i, g):
+            if g == 0:
+                q = work.tile([P, 256], U32, name="sq", align_bytes=64)
+                s = work.tile([P, 256], U8, name="ss", align_bytes=64)
+                sq[i] = (q, s)
+            q, s = sq[i]
+            nc.vector.quantize_mx(
+                out=q[:, P * g : P * (g + 1)].bitcast(FP8X4), scales=s[:, P * g : P * (g + 1)], in_=sg[i][:, H * g : H * (g + 1)]
+            )
+
         def ray_evac(i):
             t = work.tile([P, U], BF16, name="rg", align_bytes=64)
             rg[i] = t
@@ -176,9 +199,9 @@ def tile_ordinates_scattering_source_s3_kernel(
                 in_=rt[i][:].rearrange("p u r -> p r u"),
             )
 
-        def phi_pass(i, n, k):
+        def phi_pass(i, n, k, tag="acc"):
             if k == 0:
-                acc[i, n] = psum.tile([P, H], F32, name="acc", bufs=2)
+                acc[i, n] = psum.tile([P, H], F32, name=tag, bufs=2)
             cols = slice(H * n, H * (n + 1))
             if k < 2:
                 q, s = pq[i]
@@ -203,10 +226,10 @@ def tile_ordinates_scattering_source_s3_kernel(
             tt[i, n] = t
             nc.vector.tensor_tensor(out=t[:], in0=acc[i, n][:], in1=sig_t[i][:, H * n : H * (n + 1)], op=MULT)
 
-        def add_ext(i, n):
+        def add_ext(i, n, eng=None):
             t = work.tile([P, H], BF16, name="sp" + str(n), align_bytes=64)
             sp[i, n] = t
-            eng = nc.gpsimd if n == 0 else nc.vector
+            eng = eng or (nc.gpsimd if n == 0 else nc.vector)
             eng.tensor_tensor(
                 out=t[:].rearrange("p (u q e) -> p u q e", u=2, e=2),
                 in0=tt[i, n][:].rearrange("p (q u e) -> p u q e", u=2, e=2),
@@ -214,10 +237,12 @@ def tile_ordinates_scattering_source_s3_kernel(
                 op=ADD,
             )
 
-        def tr_src(i):
-            t = psum.tile([P, 4, P], F32, name="st", bufs=1)
-            st[i] = t
-            for n in range(2):
+        def tr_src(i, halves=(0, 1)):
+            if 0 in halves:
+                t = psum.tile([P, 4, P], F32, name="st", bufs=1)
+                st[i] = t
+            t = st[i]
+            for n in halves:
                 words = sp[i, n][:].bitcast(F32)
                 for u in range(2):
                     nc.tensor.transpose(t[:, 2 * n + u, :], words[:, P * u : P * (u + 1)], ident[:])
@@ -230,11 +255,21 @@ def tile_ordinates_scattering_source_s3_kernel(
                 in_=st[i][:].rearrange("p (n u) r -> p n r u", n=2),
             )
 
-        def out_mm(i, n):
-            o = psum.tile([P, H], F32, name="oacc", bufs=2)
-            oacc[i, n] = o
+        def src_evac_half(i, n, copy):
+            if n == 0:
+                t = work.tile([P, L], BF16, name="sg", align_bytes=64)
+                sg[i] = t
+            copy(
+                out=sg[i][:, H * n : H * (n + 1)].bitcast(F32).rearrange("p (r u) -> p r u", u=2),
+                in_=st[i][:, 2 * n : 2 * n + 2, :].rearrange("p u r -> p r u"),
+            )
+
+        def out_mm(i, n, gs=(0, 1), tag="oacc"):
+            if 0 in gs:
+                oacc[i, n] = psum.tile([P, H], F32, name=tag, bufs=2)
+            o = oacc[i, n]
             q, s = sq[i]
-            for g in range(2):
+            for g in gs:
                 nc.tensor.matmul_mx(
                     out=o[:],
                     lhsT=q[:, P * g : P * (g + 1)].bitcast(FP8X4),
@@ -245,12 +280,12 @@ def tile_ordinates_scattering_source_s3_kernel(
                     stop=(g == 1),
                 )
 
-        def out_evac(i, n):
+        def out_evac(i, n, copy=nc.scalar.copy):
             if n == 0:
                 t = work.tile([P, A], F32, name="ot", align_bytes=64)
                 ot[i] = t
             t = ot[i]
-            nc.scalar.copy(out=t[:, H * n : H * (n + 1)], in_=oacc[i, n][:])
+            copy(out=t[:, H * n : H * (n + 1)], in_=oacc[i, n][:])
             if i == NT - 1:
                 nc.sync.dma_start(out=out_v[:, i, H * n : H * (n + 1)], in_=t[:, H * n : H * (n + 1)])
             elif n == 1:
@@ -259,83 +294,137 @@ def tile_ordinates_scattering_source_s3_kernel(
         def ok(i):
             return 0 <= i < NT
 
-        cast(0)
+        cast_tile(0)
+        cast_part(nc.vector.tensor_copy, 0, 0, H)
+        cast_part(nc.scalar.copy, 0, H, A)
+        cast_tile(1)
+        cast_part(nc.vector.tensor_copy, 1, 0, A)
         tr_psi(0)
-        tr_ray(0)
-        scale_psi(0, 0)
-        ray_evac(0)
-        scale_psi(0, 1)
-        q_ray(0)
-        q_psi(0)
-        cast(1)
         tr_psi(1)
-        tr_ray(1)
-        ray_evac(1)
-        e_part(nc.vector.tensor_copy, 0, 0, 256)
-        e_part(nc.scalar.copy, 0, 256, 512)
+        scale_psi(0, 0)
+        scale_psi(0, 1)
         scale_psi(1, 0)
-        e_quant(0)
-        e_part(nc.vector.tensor_copy, 1, 0, 256)
-        e_part(nc.scalar.copy, 1, 256, 512)
-        scale_psi(1, 1)
-        e_quant(1)
-        q_psi(1)
-        q_ray(1)
+        q_psi(0)
+        e_part(nc.scalar.copy, 0, ES0, H)
+        tr_ray(0)
+        ray_evac(0)
+        tr_ray(1, "st")
+        ray_evac(1)
+        cast(2)
         for k in range(2):
             for n in range(2):
                 phi_pass(0, n, k)
-        for n in range(2):
-            phi_pass(0, n, 2)
-        cast(2)
+        e_part(nc.vector.tensor_copy, 0, 0, ES0)
+        scale_psi(1, 1)
+        e_quant(0)
+        q_ray(0)
+        phi_pass(0, 0, 2)
+        e_part(nc.scalar.copy, 1, ES1, H)
+        q_psi(1)
+        q_ray(1)
+        e_part(nc.vector.tensor_copy, 1, 0, ES1)
+        cast(3)
+        cast(4)
+        for k in range(2):
+            for n in range(2):
+                phi_pass(1, n, k, "oacc")
+        phi_pass(1, 0, 2)
+        mul_sigma(0, 0)
+        e_quant(1)
+        tr_psi(2)
+        phi_pass(0, 1, 2)
+        phi_pass(1, 1, 2)
+        add_ext(0, 0)
+        mul_sigma(1, 0)
+        scale_psi(2, 0)
+        mul_sigma(0, 1)
+        scale_psi(2, 1)
+        add_ext(1, 0)
+        tr_ray(2)
+        ray_evac(2)
+        mul_sigma(1, 1)
+        q_psi(2)
+        q_ray(2)
+        tr_psi(3)
+        tr_ray(3)
+        ray_evac(3)
+        scale_psi(3, 0)
+        add_ext(0, 1)
+        q_ray(3)
 
-        for s in range(NT + 3):
-            if s == 0:
-                mul_sigma(0, 0)
-                add_ext(0, 0)
-                mul_sigma(0, 1)
-                phi(1, 0)
-                phi(1, 1)
-                tr_psi(2)
-                tr_ray(2)
-                ray_evac(2)
-                cast(3)
-                scale_psi(2, 0)
-                continue
-            if ok(s + 2):
+        for s in range(2, NT - 2):
+            if s + 2 < NT:
                 tr_psi(s + 2)
                 tr_ray(s + 2)
-            if ok(s - 2):
-                tr_src(s - 2)
-            if ok(s + 1):
-                scale_psi(s + 1, 1)
-            if ok(s - 1):
-                add_ext(s - 1, 1)
-            if ok(s - 3):
+            tr_src(s - 2)
+            scale_psi(s + 1, 1)
+            add_ext(s - 1, 1)
+            if s > 2:
                 out_evac(s - 3, 1)
-            if ok(s + 2):
-                ray_evac(s + 2)
-            if ok(s + 1):
-                q_psi(s + 1)
-            if s == 1:
-                q_ray(2)
-            if ok(s + 2):
-                q_ray(s + 2)
-            if ok(s - 2):
-                src_evac(s - 2)
-                q_src(s - 2)
-            if ok(s) and s > 1:
-                phi(s, 0)
-                phi(s, 1)
-            if ok(s + 3):
+            ray_evac(s + 2)
+            q_psi(s + 1)
+            q_ray(s + 2)
+            src_evac(s - 2)
+            q_src(s - 2)
+            phi(s, 0)
+            phi(s, 1)
+            if s + 3 < NT:
                 cast(s + 3)
-            if ok(s):
-                mul_sigma(s, 0)
-                add_ext(s, 0)
-            if ok(s + 2):
-                scale_psi(s + 2, 0)
-            if ok(s):
-                mul_sigma(s, 1)
-            if ok(s - 2):
-                out_mm(s - 2, 0)
-                out_mm(s - 2, 1)
-                out_evac(s - 2, 0)
+            mul_sigma(s, 0)
+            add_ext(s, 0)
+            scale_psi(s + 2, 0)
+            mul_sigma(s, 1)
+            out_mm(s - 2, 0)
+            out_mm(s - 2, 1)
+            out_evac(s - 2, 0)
+
+        a, b = NT - 2, NT - 1
+        tr_src(a - 2)
+        scale_psi(b, 1)
+        add_ext(a - 1, 1)
+        out_evac(a - 3, 1)
+        q_psi(b)
+        src_evac(a - 2)
+        q_src(a - 2)
+        phi(a, 0)
+        phi(a, 1)
+        mul_sigma(a, 0)
+        add_ext(a, 0)
+        mul_sigma(a, 1)
+        tr_src(a - 1)
+        src_evac(a - 1)
+        out_mm(a - 2, 0)
+        out_mm(a - 2, 1)
+        add_ext(a, 1)
+        q_src(a - 1)
+        phi(b, 0)
+        phi(b, 1)
+        out_evac(a - 2, 0)
+        out_evac(a - 2, 1)
+        mul_sigma(b, 0)
+        tr_src(a)
+        add_ext(b, 0, nc.vector)
+        src_evac(a)
+        mul_sigma(b, 1)
+        out_mm(a - 1, 0)
+        out_mm(a - 1, 1)
+        add_ext(b, 1)
+        q_src(a)
+        tr_src(b, (0,))
+        out_evac(a - 1, 0)
+        src_evac_half(b, 0, nc.scalar.copy)
+        q_src_half(b, 0)
+        tr_src(b, (1,))
+        src_evac_half(b, 1, nc.vector.tensor_copy)
+        out_evac(a - 1, 1)
+        out_mm(a, 0)
+        out_mm(a, 1)
+        q_src_half(b, 1)
+        out_mm(b, 0, (0,), "pt")
+        out_mm(b, 1, (0,), "pt")
+        out_mm(b, 0, (1,), "pt")
+        out_mm(b, 1, (1,), "pt")
+        out_evac(a, 0)
+        out_evac(a, 1, nc.vector.tensor_copy)
+        out_evac(b, 0)
+        out_evac(b, 1, nc.vector.tensor_copy)

@@ -138,20 +138,35 @@ def tile_ordinates_scattering_source_s3_kernel(
             cast_tile(i)
             cast_part(nc.scalar.copy, i, 0, A)
 
+        pp, rp = {}, {}
+
+        def perm_psi(i):
+            t = work.tile([P, 2, 2, P], F32, name="pp", align_bytes=64)
+            pp[i] = t
+            nc.scalar.copy(out=t[:], in_=pb[i][:].bitcast(F32).rearrange("p (g q u) -> p g u q", g=2, u=2))
+
+        def perm_ray(i):
+            t = work.tile([P, 2, P], F32, name="rp", align_bytes=64)
+            rp[i] = t
+            nc.vector.tensor_copy(out=t[:], in_=ray_t[i].bitcast(F32).rearrange("p (q u) -> p u q", u=2))
+
         def tr_psi(i):
             t = psum.tile([P, 4, P], F32, name="pt", bufs=2)
             pt[i] = t
-            words = pb[i][:].bitcast(F32)
             for g in range(2):
                 for u in range(2):
-                    nc.tensor.transpose(t[:, 2 * g + u, :], words[:, 256 * g + u : 256 * (g + 1) : 2], ident[:])
+                    if i in pp:
+                        w = pp[i][:, g, u, :]
+                    else:
+                        w = pb[i][:].bitcast(F32)[:, 256 * g + u : 256 * (g + 1) : 2]
+                    nc.tensor.transpose(t[:, 2 * g + u, :], w, ident[:])
 
         def tr_ray(i, tag="rt"):
             t = psum.tile([P, 2, P], F32, name=tag, bufs=1)
             rt[i] = t
-            words = ray_t[i].bitcast(F32)
             for u in range(2):
-                nc.tensor.transpose(t[:, u, :], words[:, u:256:2], ident[:])
+                w = rp[i][:, u, :] if i in rp else ray_t[i].bitcast(F32)[:, u:256:2]
+                nc.tensor.transpose(t[:, u, :], w, ident[:])
 
         def scale_psi(i, g):
             if g == 0:
@@ -285,10 +300,15 @@ def tile_ordinates_scattering_source_s3_kernel(
                 t = work.tile([P, A], F32, name="ot", align_bytes=64)
                 ot[i] = t
             t = ot[i]
-            copy(out=t[:, H * n : H * (n + 1)], in_=oacc[i, n][:])
-            if i == NT - 1:
-                nc.sync.dma_start(out=out_v[:, i, H * n : H * (n + 1)], in_=t[:, H * n : H * (n + 1)])
-            elif n == 1:
+            parts = 2 if (i, n) == (NT - 1, 1) else 1
+            w = H // parts
+            for k in range(parts):
+                cols = slice(H * n + w * k, H * n + w * (k + 1))
+                copy(out=t[:, cols], in_=oacc[i, n][:, w * k : w * (k + 1)])
+                if i == NT - 1:
+                    queue = nc.scalar if k == 1 else nc.sync
+                    queue.dma_start(out=out_v[:, i, cols], in_=t[:, cols])
+            if i < NT - 1 and n == 1:
                 nc.sync.dma_start(out=out_v[:, i, :], in_=t[:])
 
         def ok(i):
@@ -321,16 +341,16 @@ def tile_ordinates_scattering_source_s3_kernel(
         phi_pass(0, 0, 2)
         e_part(nc.scalar.copy, 1, ES1, H)
         q_psi(1)
-        q_ray(1)
         e_part(nc.vector.tensor_copy, 1, 0, ES1)
+        q_ray(1)
         cast(3)
         cast(4)
         for k in range(2):
             for n in range(2):
                 phi_pass(1, n, k, "oacc")
         phi_pass(1, 0, 2)
-        mul_sigma(0, 0)
         e_quant(1)
+        mul_sigma(0, 0)
         tr_psi(2)
         phi_pass(0, 1, 2)
         phi_pass(1, 1, 2)
@@ -351,6 +371,7 @@ def tile_ordinates_scattering_source_s3_kernel(
         scale_psi(3, 0)
         add_ext(0, 1)
         q_ray(3)
+        cast(5)
 
         for s in range(2, NT - 2):
             if s + 2 < NT:
@@ -364,18 +385,22 @@ def tile_ordinates_scattering_source_s3_kernel(
             ray_evac(s + 2)
             q_psi(s + 1)
             q_ray(s + 2)
+            if s + 3 < NT:
+                perm_ray(s + 3)
             src_evac(s - 2)
             q_src(s - 2)
             phi(s, 0)
             phi(s, 1)
-            if s + 3 < NT:
-                cast(s + 3)
+            if s + 4 < NT:
+                cast(s + 4)
             mul_sigma(s, 0)
             add_ext(s, 0)
             scale_psi(s + 2, 0)
             mul_sigma(s, 1)
             out_mm(s - 2, 0)
             out_mm(s - 2, 1)
+            if s + 4 < NT:
+                perm_psi(s + 4)
             out_evac(s - 2, 0)
 
         a, b = NT - 2, NT - 1

@@ -370,81 +370,90 @@ def tile_ordinates_scattering_source_s3_kernel(
         ray_evac(3)
         scale_psi(3, 0)
         add_ext(0, 1)
-        q_ray(3)
         cast(5)
 
         for s in range(2, NT - 2):
-            if s + 2 < NT:
-                tr_psi(s + 2)
-                tr_ray(s + 2)
-            tr_src(s - 2)
+            tr_psi(s + 2)
+            tr_ray(s + 2)
+            if s > 2:
+                tr_src(s - 2)
             scale_psi(s + 1, 1)
             add_ext(s - 1, 1)
-            if s > 2:
-                out_evac(s - 3, 1)
+            if s >= 4:
+                out_evac(s - 4, 1)
             ray_evac(s + 2)
             q_psi(s + 1)
-            q_ray(s + 2)
-            if s + 3 < NT:
-                perm_ray(s + 3)
+            q_ray(s + 1)
+            if s >= 3:
+                q_src(s - 3)
+            if s == 2:
+                phi(2, 0)
+                phi(2, 1)
+                tr_src(0)
             src_evac(s - 2)
-            q_src(s - 2)
-            phi(s, 0)
-            phi(s, 1)
+            if s > 2:
+                phi(s, 0)
+                phi(s, 1)
             if s + 4 < NT:
                 cast(s + 4)
             mul_sigma(s, 0)
             add_ext(s, 0)
             scale_psi(s + 2, 0)
             mul_sigma(s, 1)
-            out_mm(s - 2, 0)
-            out_mm(s - 2, 1)
             if s + 4 < NT:
                 perm_psi(s + 4)
-            out_evac(s - 2, 0)
+            if s >= 3:
+                out_mm(s - 3, 0)
+                out_mm(s - 3, 1)
+                out_evac(s - 3, 0)
 
         a, b = NT - 2, NT - 1
         tr_src(a - 2)
         scale_psi(b, 1)
         add_ext(a - 1, 1)
-        out_evac(a - 3, 1)
+        out_evac(a - 4, 1)
         q_psi(b)
+        q_ray(b)
+        q_src(a - 3)
         src_evac(a - 2)
-        q_src(a - 2)
         phi(a, 0)
         phi(a, 1)
         mul_sigma(a, 0)
         add_ext(a, 0)
         mul_sigma(a, 1)
         tr_src(a - 1)
-        src_evac(a - 1)
-        out_mm(a - 2, 0)
-        out_mm(a - 2, 1)
+        out_mm(a - 3, 0)
+        out_mm(a - 3, 1)
+        q_src(a - 2)
         add_ext(a, 1)
-        q_src(a - 1)
+        src_evac(a - 1)
+        out_evac(a - 3, 0)
         phi(b, 0)
         phi(b, 1)
+        out_evac(a - 3, 1)
+        out_mm(a - 2, 0)
+        out_mm(a - 2, 1)
+        mul_sigma(b, 0)
+        q_src(a - 1)
+        add_ext(b, 0, nc.vector)
+        mul_sigma(b, 1)
+        tr_src(a)
         out_evac(a - 2, 0)
         out_evac(a - 2, 1)
-        mul_sigma(b, 0)
-        tr_src(a)
-        add_ext(b, 0, nc.vector)
         src_evac(a)
-        mul_sigma(b, 1)
-        out_mm(a - 1, 0)
-        out_mm(a - 1, 1)
+        out_mm(a - 1, 0, (0, 1), "pt")
+        out_mm(a - 1, 1, (0, 1), "pt")
         add_ext(b, 1)
         q_src(a)
-        tr_src(b, (0,))
-        out_evac(a - 1, 0)
+        tr_src(b)
         src_evac_half(b, 0, nc.scalar.copy)
-        q_src_half(b, 0)
-        tr_src(b, (1,))
         src_evac_half(b, 1, nc.vector.tensor_copy)
-        out_evac(a - 1, 1)
+        q_src_half(b, 0)
+        q_src_half(b, 1)
+        out_evac(a - 1, 0)
+        out_evac(a - 1, 1, nc.vector.tensor_copy)
         out_mm(a, 0)
         out_mm(a, 1)
-        q_src_half(b, 1)
         out_mm(b, 0, (0,), "pt")
         out_mm(b, 1, (0,), "pt")
         out_mm(b, 0, (1,), "pt")

from contextlib import ExitStack

import concourse.mybir as mybir
from concourse.masks import make_identity

C, A, U, L = 1536, 1024, 512, 1024
FLOPS = 2 * C * L * (A + U + A)

F32 = mybir.dt.float32
BF16 = mybir.dt.bfloat16
U32 = mybir.dt.uint32
I32 = mybir.dt.int32
U8 = mybir.dt.uint8
E4M3 = mybir.dt.float8_e4m3fn
FP8X4 = mybir.dt.float8_e4m3fn_x4
FP4X4 = mybir.dt.float4_e2m1fn_x4
MULT = mybir.AluOpType.mult
ADD = mybir.AluOpType.add

P = 128
NT = C // P
ES0 = 256
ES1 = 320
H = 512


def tile_ordinates_scattering_source_s3_kernel(
    tc, psi_bytes, psi_scale, ray, d_words, d_scales, e, sigma, ext, m_words, m_scales, out
):
    nc = tc.nc
    psi_v = psi_bytes.rearrange("(p i) a -> p i a", i=NT)
    ray_v = ray.rearrange("(p i) a -> p i a", i=NT)
    sig_v = sigma.rearrange("(p i) a -> p i a", i=NT)
    ext_v = ext.rearrange("(p i) a -> p i a", i=NT)
    out_v = out.rearrange("(p i) a -> p i a", i=NT)
    e_v = e.rearrange("(p j) n -> p j n", j=4)

    with ExitStack() as ctx:
        keep = ctx.enter_context(tc.tile_pool(name="keep", bufs=1))
        work = ctx.enter_context(tc.tile_pool(name="work", bufs=4))
        psum = ctx.enter_context(tc.psum_pool(name="psum", bufs=1))
        ctx.enter_context(tc.manual_schedule())

        sc = keep.tile([P, 2, 4], F32, name="sc")
        nc.scalar.dma_start(out=sc[:], in_=psi_scale.rearrange("o (g p t) -> p (o g) t", p=P, t=4))
        ident = keep.tile([P, P], F32, name="ident")
        make_identity(nc, ident[:])
        warm = keep.tile([P, 8], F32, name="warm")
        nc.gpsimd.memset(warm[:], 0.0)
        warm2 = keep.tile([P, 8], F32, name="warm2")
        nc.scalar.copy(out=warm2[:], in_=warm[:])

        ds = keep.tile([P, 2, L], U8, name="ds", align_bytes=256)
        ms = keep.tile([P, 2, A], U8, name="ms", align_bytes=256)
        nc.vector.memset(ds[:].bitcast(I32), 0)
        nc.vector.memset(ms[:].bitcast(I32), 0)

        psi_t, ray_t, sig_t, ext_t = {}, {}, {}, {}

        def load(store, view, dt, width, i0, n, nm):
            t = keep.tile([P, n, width], dt, name=nm + str(i0), align_bytes=64)
            nc.sync.dma_start(out=t[:], in_=view[:, i0 : i0 + n, :])
            for k in range(n):
                store[i0 + k] = t[:, k, :]

        def load_psi(i0, n):
            load(psi_t, psi_v, U8, A, i0, n, "psib")

        def load_ray(i0, n):
            load(ray_t, ray_v, BF16, U, i0, n, "ray")

        def load_se(i0, n):
            load(sig_t, sig_v, BF16, L, i0, n, "sig")
            load(ext_t, ext_v, BF16, L, i0, n, "ext")

        def load_scales(t, src):
            for q in range(4):
                nc.sync.dma_start(
                    out=t[32 * q : 32 * q + 4, :, :].bitcast(I32),
                    in_=src[:, 4 * q : 4 * q + 4, :].rearrange("g q n -> q g n").bitcast(I32),
                )

        load_psi(0, 2)
        load_scales(ds, d_scales)
        dw = keep.tile([P, 2, 2 * L], U8, name="dw", align_bytes=256)
        nc.sync.dma_start(out=dw[:], in_=d_words.rearrange("g p n -> p g n"))
        e_raw = []

        def load_e(h):
            t = keep.tile([P, 4, H], BF16, name="eraw" + str(h), align_bytes=64)
            nc.sync.dma_start(out=t[:], in_=e_v[:, :, H * h : H * (h + 1)])
            e_raw.append(t)

        load_e(0)
        load_ray(0, 2)
        load_psi(2, 2)
        load_e(1)
        load_se(0, 1)
        load_ray(2, 2)
        load_se(1, 1)
        load_psi(4, 2)
        load_ray(4, 2)
        mw = keep.tile([P, 2, 2 * A], U8, name="mw", align_bytes=256)
        nc.sync.dma_start(out=mw[:], in_=m_words.rearrange("g p n -> p g n"))
        load_scales(ms, m_scales)
        load_se(2, 2)
        load_psi(6, 2)
        load_ray(6, 2)
        load_se(4, 2)
        load_psi(8, 4)
        load_ray(8, 4)
        for i in range(6, NT, 2):
            load_se(i, 2)

        eq = [keep.tile([P, H], U32, name="eq" + str(h), align_bytes=256) for h in range(2)]
        es = [keep.tile([P, H], U8, name="es" + str(h), align_bytes=256) for h in range(2)]
        eg = [keep.tile([P, 4 * H], BF16, name="eg" + str(h), align_bytes=256) for h in range(2)]

        def e_part(copy, h, c0, c1):
            copy(
                out=eg[h][:, 4 * c0 : 4 * c1].rearrange("p (c i t) -> p c t i", i=4, t=4),
                in_=e_raw[h][:, :, c0:c1].rearrange("p t (c i) -> p c t i", i=4),
            )

        def e_quant(h):
            nc.vector.quantize_mx(out=eq[h][:].bitcast(FP8X4), scales=es[h][:], in_=eg[h][:])

        pb, pt, pg, pq, rt, rg, rq, acc, tt, sp, st, sg, sq, oacc, ot = ({} for x in range(15))

        def cast_tile(i):
            t = work.tile([P, A], BF16, name="pb", align_bytes=64)
            pb[i] = t

        def cast_part(copy, i, a, b):
            copy(out=pb[i][:, a:b], in_=psi_t[i][:, a:b].bitcast(E4M3))

        def cast(i):
            cast_tile(i)
            cast_part(nc.scalar.copy, i, 0, A)

        pp, rp = {}, {}

        def perm_psi(i):
            t = work.tile([P, 2, 2, P], F32, name="pp", align_bytes=64)
            pp[i] = t
            nc.scalar.copy(out=t[:], in_=pb[i][:].bitcast(F32).rearrange("p (g q u) -> p g u q", g=2, u=2))

        def perm_ray(i):
            t = work.tile([P, 2, P], F32, name="rp", align_bytes=64)
            rp[i] = t
            nc.vector.tensor_copy(out=t[:], in_=ray_t[i].bitcast(F32).rearrange("p (q u) -> p u q", u=2))

        def tr_psi(i):
            t = psum.tile([P, 4, P], F32, name="pt", bufs=2)
            pt[i] = t
            for g in range(2):
                for u in range(2):
                    if i in pp:
                        w = pp[i][:, g, u, :]
                    else:
                        w = pb[i][:].bitcast(F32)[:, 256 * g + u : 256 * (g + 1) : 2]
                    nc.tensor.transpose(t[:, 2 * g + u, :], w, ident[:])

        def tr_ray(i, tag="rt"):
            t = psum.tile([P, 2, P], F32, name=tag, bufs=1)
            rt[i] = t
            for u in range(2):
                w = rp[i][:, u, :] if i in rp else ray_t[i].bitcast(F32)[:, u:256:2]
                nc.tensor.transpose(t[:, u, :], w, ident[:])

        def scale_psi(i, g):
            if g == 0:
                t = work.tile([P, 2, H], BF16, name="pg", align_bytes=64)
                pg[i] = t
            t = pg[i]
            bank = pt[i][:].rearrange("p s r -> p (s r)").bitcast(BF16)
            nc.vector.tensor_tensor(
                out=t[:, g, :].rearrange("p (r u e) -> p r u e", u=2, e=2),
                in0=bank[:, H * g : H * (g + 1)].rearrange("p (u r e) -> p r u e", u=2, e=2),
                in1=sc[:, g, :].unsqueeze(1).to_broadcast([P, P, 4]).rearrange("p r (u e) -> p r u e", u=2, e=2),
                op=MULT,
            )

        def quant(store, i, src, words, nm):
            q = work.tile([P, words], U32, name=nm + "q", align_bytes=64)
            s = work.tile([P, words], U8, name=nm + "s", align_bytes=64)
            store[i] = (q, s)
            nc.vector.quantize_mx(out=q[:].bitcast(FP8X4), scales=s[:], in_=src)

        def q_psi(i):
            quant(pq, i, pg[i][:].rearrange("p g n -> p (g n)"), 256, "p")

        def q_ray(i):
            quant(rq, i, rg[i][:], 128, "r")

        def q_src(i):
            quant(sq, i, sg[i][:], 256, "s")

        def q_src_half(i, g):
            if g == 0:
                q = work.tile([P, 256], U32, name="sq", align_bytes=64)
                s = work.tile([P, 256], U8, name="ss", align_bytes=64)
                sq[i] = (q, s)
            q, s = sq[i]
            nc.vector.quantize_mx(
                out=q[:, P * g : P * (g + 1)].bitcast(FP8X4), scales=s[:, P * g : P * (g + 1)], in_=sg[i][:, H * g : H * (g + 1)]
            )

        def ray_evac(i):
            t = work.tile([P, U], BF16, name="rg", align_bytes=64)
            rg[i] = t
            nc.scalar.copy(
                out=t[:].bitcast(F32).rearrange("p (r u) -> p r u", u=2),
                in_=rt[i][:].rearrange("p u r -> p r u"),
            )

        def phi_pass(i, n, k, tag="acc"):
            if k == 0:
                acc[i, n] = psum.tile([P, H], F32, name=tag, bufs=2)
            cols = slice(H * n, H * (n + 1))
            if k < 2:
                q, s = pq[i]
                lq, ls = q[:, P * k : P * (k + 1)], s[:, P * k : P * (k + 1)]
                r = dw[:, k, 2 * H * n : 2 * H * (n + 1)].bitcast(FP4X4)
                rs = ds[:, k, cols]
            else:
                q, s = rq[i]
                lq, ls = q[:], s[:]
                r = eq[n][:].bitcast(FP8X4)
                rs = es[n][:]
            nc.tensor.matmul_mx(
                out=acc[i, n][:], lhsT=lq.bitcast(FP8X4), lhsT_scale=ls, rhs=r, rhs_scale=rs, start=(k == 0), stop=(k == 2)
            )

        def phi(i, n):
            for k in range(3):
                phi_pass(i, n, k)

        def mul_sigma(i, n):
            t = work.tile([P, H], F32, name="t" + str(n), align_bytes=64)
            tt[i, n] = t
            nc.vector.tensor_tensor(out=t[:], in0=acc[i, n][:], in1=sig_t[i][:, H * n : H * (n + 1)], op=MULT)

        def add_ext(i, n, eng=None):
            t = work.tile([P, H], BF16, name="sp" + str(n), align_bytes=64)
            sp[i, n] = t
            eng = eng or (nc.gpsimd if n == 0 else nc.vector)
            eng.tensor_tensor(
                out=t[:].rearrange("p (u q e) -> p u q e", u=2, e=2),
                in0=tt[i, n][:].rearrange("p (q u e) -> p u q e", u=2, e=2),
                in1=ext_t[i][:, H * n : H * (n + 1)].rearrange("p (q u e) -> p u q e", u=2, e=2),
                op=ADD,
            )

        def tr_src(i, halves=(0, 1)):
            if 0 in halves:
                t = psum.tile([P, 4, P], F32, name="st", bufs=1)
                st[i] = t
            t = st[i]
            for n in halves:
                words = sp[i, n][:].bitcast(F32)
                for u in range(2):
                    nc.tensor.transpose(t[:, 2 * n + u, :], words[:, P * u : P * (u + 1)], ident[:])

        def src_evac(i):
            t = work.tile([P, L], BF16, name="sg", align_bytes=64)
            sg[i] = t
            nc.scalar.copy(
                out=t[:].bitcast(F32).rearrange("p (n r u) -> p n r u", n=2, u=2),
                in_=st[i][:].rearrange("p (n u) r -> p n r u", n=2),
            )

        def src_evac_half(i, n, copy):
            if n == 0:
                t = work.tile([P, L], BF16, name="sg", align_bytes=64)
                sg[i] = t
            copy(
                out=sg[i][:, H * n : H * (n + 1)].bitcast(F32).rearrange("p (r u) -> p r u", u=2),
                in_=st[i][:, 2 * n : 2 * n + 2, :].rearrange("p u r -> p r u"),
            )

        def out_mm(i, n, gs=(0, 1), tag="oacc"):
            if 0 in gs:
                oacc[i, n] = psum.tile([P, H], F32, name=tag, bufs=2)
            o = oacc[i, n]
            q, s = sq[i]
            for g in gs:
                nc.tensor.matmul_mx(
                    out=o[:],
                    lhsT=q[:, P * g : P * (g + 1)].bitcast(FP8X4),
                    lhsT_scale=s[:, P * g : P * (g + 1)],
                    rhs=mw[:, g, 2 * H * n : 2 * H * (n + 1)].bitcast(FP4X4),
                    rhs_scale=ms[:, g, H * n : H * (n + 1)],
                    start=(g == 0),
                    stop=(g == 1),
                )

        def out_evac(i, n, copy=nc.scalar.copy):
            if n == 0:
                t = work.tile([P, A], F32, name="ot", align_bytes=64)
                ot[i] = t
            t = ot[i]
            parts = 2 if (i, n) == (NT - 1, 1) else 1
            w = H // parts
            for k in range(parts):
                cols = slice(H * n + w * k, H * n + w * (k + 1))
                copy(out=t[:, cols], in_=oacc[i, n][:, w * k : w * (k + 1)])
                if i == NT - 1:
                    queue = nc.scalar if k == 1 else nc.sync
                    queue.dma_start(out=out_v[:, i, cols], in_=t[:, cols])
            if i < NT - 1 and n == 1:
                nc.sync.dma_start(out=out_v[:, i, :], in_=t[:])

        def ok(i):
            return 0 <= i < NT

        cast_tile(0)
        cast_part(nc.vector.tensor_copy, 0, 0, H)
        cast_part(nc.scalar.copy, 0, H, A)
        cast_tile(1)
        cast_part(nc.vector.tensor_copy, 1, 0, A)
        tr_psi(0)
        tr_psi(1)
        scale_psi(0, 0)
        scale_psi(0, 1)
        scale_psi(1, 0)
        q_psi(0)
        e_part(nc.scalar.copy, 0, ES0, H)
        tr_ray(0)
        ray_evac(0)
        tr_ray(1, "st")
        ray_evac(1)
        cast(2)
        for k in range(2):
            for n in range(2):
                phi_pass(0, n, k)
        e_part(nc.vector.tensor_copy, 0, 0, ES0)
        scale_psi(1, 1)
        e_quant(0)
        q_ray(0)
        phi_pass(0, 0, 2)
        e_part(nc.scalar.copy, 1, ES1, H)
        q_psi(1)
        e_part(nc.vector.tensor_copy, 1, 0, ES1)
        q_ray(1)
        cast(3)
        cast(4)
        for k in range(2):
            for n in range(2):
                phi_pass(1, n, k, "oacc")
        phi_pass(1, 0, 2)
        e_quant(1)
        mul_sigma(0, 0)
        tr_psi(2)
        phi_pass(0, 1, 2)
        phi_pass(1, 1, 2)
        add_ext(0, 0)
        mul_sigma(1, 0)
        scale_psi(2, 0)
        mul_sigma(0, 1)
        scale_psi(2, 1)
        add_ext(1, 0)
        tr_ray(2)
        ray_evac(2)
        mul_sigma(1, 1)
        q_psi(2)
        q_ray(2)
        tr_psi(3)
        tr_ray(3)
        ray_evac(3)
        scale_psi(3, 0)
        add_ext(0, 1)
        cast(5)

        for s in range(2, NT - 2):
            tr_psi(s + 2)
            tr_ray(s + 2)
            if s > 2:
                tr_src(s - 2)
            scale_psi(s + 1, 1)
            add_ext(s - 1, 1)
            if s >= 4:
                out_evac(s - 4, 1)
            ray_evac(s + 2)
            q_psi(s + 1)
            q_ray(s + 1)
            if s >= 3:
                q_src(s - 3)
            if s == 2:
                phi(2, 0)
                phi(2, 1)
                tr_src(0)
            src_evac(s - 2)
            if s > 2:
                phi(s, 0)
                phi(s, 1)
            if s + 4 < NT:
                cast(s + 4)
            mul_sigma(s, 0)
            add_ext(s, 0)
            scale_psi(s + 2, 0)
            mul_sigma(s, 1)
            if s + 4 < NT:
                perm_psi(s + 4)
            if s >= 3:
                out_mm(s - 3, 0)
                out_mm(s - 3, 1)
                out_evac(s - 3, 0)

        a, b = NT - 2, NT - 1
        tr_src(a - 2)
        scale_psi(b, 1)
        add_ext(a - 1, 1)
        out_evac(a - 4, 1)
        q_psi(b)
        q_ray(b)
        q_src(a - 3)
        src_evac(a - 2)
        phi(a, 0)
        phi(a, 1)
        mul_sigma(a, 0)
        add_ext(a, 0)
        mul_sigma(a, 1)
        tr_src(a - 1)
        out_mm(a - 3, 0)
        out_mm(a - 3, 1)
        q_src(a - 2)
        add_ext(a, 1)
        src_evac(a - 1)
        out_evac(a - 3, 0)
        phi(b, 0)
        phi(b, 1)
        out_evac(a - 3, 1)
        out_mm(a - 2, 0)
        out_mm(a - 2, 1)
        mul_sigma(b, 0)
        q_src(a - 1)
        add_ext(b, 0, nc.vector)
        mul_sigma(b, 1)
        tr_src(a)
        out_evac(a - 2, 0)
        out_evac(a - 2, 1)
        src_evac(a)
        out_mm(a - 1, 0, (0, 1), "pt")
        out_mm(a - 1, 1, (0, 1), "pt")
        add_ext(b, 1)
        q_src(a)
        tr_src(b)
        src_evac_half(b, 0, nc.scalar.copy)
        src_evac_half(b, 1, nc.vector.tensor_copy)
        q_src_half(b, 0)
        q_src_half(b, 1)
        out_evac(a - 1, 0)
        out_evac(a - 1, 1, nc.vector.tensor_copy)
        out_mm(a, 0)
        out_mm(a, 1)
        out_mm(b, 0, (0,), "pt")
        out_mm(b, 1, (0,), "pt")
        out_mm(b, 0, (1,), "pt")
        out_mm(b, 1, (1,), "pt")
        out_evac(a, 0)
        out_evac(a, 1, nc.vector.tensor_copy)
        out_evac(b, 0)
        out_evac(b, 1, nc.vector.tensor_copy)
